import numpy as np
import ml_dtypes


def mxq(x, axis, fmt="e4m3"):
    dtype, down = {"e4m3": (ml_dtypes.float8_e4m3fn, 7), "e5m2": (ml_dtypes.float8_e5m2, 14)}[fmt]
    v = np.moveaxis(np.asarray(x, np.float32).astype(ml_dtypes.bfloat16).astype(np.float64), axis, -1)
    blocks = v.reshape(v.shape[:-1] + (-1, 32))
    amax = np.abs(blocks).max(-1, keepdims=True)
    byte = np.maximum(np.where(amax > 0, np.frexp(amax)[1] - 1 + 127, 0) - down, 1)
    scale = np.exp2(byte - 127.0)
    codes = (blocks / scale).astype(np.float32).astype(dtype).astype(np.float64)
    return np.moveaxis((codes * scale).reshape(v.shape), -1, axis)


WIDE = False


def mx_kscale(k):
    if not WIDE:
        return np.ones(k)
    levels = np.array([10, -10, 5, -5, 0])
    if k % 512:
        return np.exp2(np.random.permutation(np.resize(levels, k // 32))).repeat(32)
    a = np.empty((k // 512, 16))
    for p in range(k // 512):
        a[p, :8] = np.random.permutation(np.resize(levels, 8))
        for g in range(8):
            far = levels[np.abs(levels - a[p, g]) >= 10]
            a[p, g + 8] = far[np.random.randint(len(far))]
    return np.exp2(a.ravel()).repeat(32)


def f64(x):
    return np.asarray(x).astype(np.float64)


def striped(idx):
    return np.tile(np.asarray(idx).reshape(-1, 16).T, (8, 1)).astype(np.uint16)


def unstriped(offs):
    return offs[:16].T.reshape(-1).astype(np.int64)


E2M1 = np.array([0.0, 0.5, 1.0, 1.5, 2.0, 3.0, 4.0, 6.0, -0.0, -0.5, -1.0, -1.5, -2.0, -3.0, -4.0, -6.0])


def pack_weight(w, fmt):
    k, n = w.shape
    w = f64(np.asarray(w, np.float32).astype(ml_dtypes.bfloat16)).reshape(k // 32, 32, n)
    amax = np.abs(w).max(1)
    if fmt == "e4m3":
        byte = np.frexp(amax)[1] - 1 + 127 - 7
    else:
        mant, ex = np.frexp(amax / 6.0)
        byte = np.where(mant > 0.5, ex, ex - 1) + 127
    byte = np.clip(np.where(amax > 0, byte, 1), 1, 254)
    scaled = (w * np.exp2(127.0 - byte)[:, None, :]).reshape(k, n).astype(np.float32)
    by_word = np.ascontiguousarray(scaled.reshape(k // 512, 128, 4, n).transpose(0, 1, 3, 2))
    if fmt == "e4m3":
        words = by_word.astype(ml_dtypes.float8_e4m3fn).view(np.uint8)
    else:
        c = by_word.astype(ml_dtypes.float4_e2m1fn).view(np.uint8) & 0xF
        words = (c[..., 0::2] | (c[..., 1::2] << 4)).reshape(k // 512, 128, 2 * n)
    return np.ascontiguousarray(words), np.ascontiguousarray(byte.astype(np.uint8).reshape(k // 512, 16, n))


def unpack_weight(words, scales, fmt):
    g, _, n = scales.shape
    words = np.ascontiguousarray(words).reshape(g, 128, n, -1)
    if fmt == "e4m3":
        vals = words.view(ml_dtypes.float8_e4m3fn).astype(np.float64)
    else:
        nib = np.empty((g, 128, n, 4), np.uint8)
        nib[..., 0::2] = words & 0xF
        nib[..., 1::2] = words >> 4
        vals = E2M1[nib]
    vals = vals * np.repeat(np.exp2(scales.astype(np.float64) - 127.0), 8, axis=1)[..., None]
    return vals.transpose(0, 1, 3, 2).reshape(g * 512, n)


def sigmoid(v):
    return 1.0 / (1.0 + np.exp(-v))


def bf(x):
    return np.asarray(x, np.float32).astype(ml_dtypes.bfloat16)


def planes(Y):
    r, m = Y.shape
    b = f64(bf(Y)).reshape(r // 32, 32, m)
    amax = np.abs(b).max(1)
    byte = np.clip(np.where(amax > 0, np.frexp(amax)[1] - 1 + 127 - 7, 1), 1, 254)
    codes = (b * np.exp2(127.0 - byte)[:, None, :]).reshape(r, m).astype(np.float32).astype(ml_dtypes.float8_e4m3fn).view(np.uint8)
    words = codes.reshape(r // 512, 128, 4, m).transpose(0, 1, 3, 2)
    return np.ascontiguousarray(words), np.ascontiguousarray(byte.astype(np.uint8).reshape(r // 512, 16, m))


D, T, I, Q, E, U, M = 512, 2048, 512, 512, 512, 1024, 1024


def setup_inputs():
    n = np.random.standard_normal
    idx = np.random.permutation(T)[:I]
    idx2 = np.random.permutation(U)[:Q]
    idx3 = np.random.permutation(U)[:Q]
    idx4 = np.random.permutation(M)[:I]
    fd = mx_kscale(D)
    fq = mx_kscale(Q)
    keysp = pack_weight(n((D, T)) / fd[:, None], "e2m1")
    return {
        "users": (n((D, U)) * 1.0 / np.sqrt(D) * fd[:, None]).astype(np.float32),
        "keys_words": keysp[0],
        "keys_scales": keysp[1],
        "qs": (np.random.uniform(0.5, 2.0, (Q, 1)) * fq[:, None]).astype(np.float32),
        "msgs": (n((Q, E)) * 1 / np.sqrt(Q) / fq[:, None]).astype(np.float32),
        "old": (n((E, M)) * 1.0).astype(np.float32),
        "offs": striped(idx),
        "offs2": striped(idx2),
        "offs3": striped(idx3),
        "offs4": striped(idx4),
    }


def reference(users, keys_words, keys_scales, qs, msgs, old, offs, offs2, offs3, offs4):
    idx = unstriped(offs)
    idx2 = unstriped(offs2)
    idx3 = unstriped(offs3)
    idx4 = unstriped(offs4)
    keysu = unpack_weight(keys_words, keys_scales, "e2m1")
    usersidx2q = mxq(f64(users)[:, idx2], 0, "e4m3")
    keysidxg = keysu[:, idx]
    a = usersidx2q.T @ keysidxg
    usersidx3q = mxq(f64(users)[:, idx3], 0, "e4m3")
    b = usersidx3q.T @ keysidxg
    s = np.maximum(a, b)
    w = sigmoid(s)
    wq = w * f64(qs)
    msgsq = mxq(f64(msgs), 0, "e4m3")
    wqq = mxq(wq, 0, "e4m3")
    dl = msgsq.T @ wqq
    df = np.zeros((E, M))
    df[:, idx4] = dl
    y = f64(old) + df
    words, scales = planes(y)
    return y, words, scales

@@ -1,0 +1,255 @@
+from contextlib import ExitStack
+
+import concourse.mybir as mybir
+
+D, T, I, Q, E, U, M = 512, 2048, 512, 512, 512, 1024, 1024
+FLOPS = 2 * (2 * Q * I * D + E * I * Q)
+
+F32 = mybir.dt.float32
+BF16 = mybir.dt.bfloat16
+I32 = mybir.dt.int32
+U32 = mybir.dt.uint32
+U16 = mybir.dt.uint16
+U8 = mybir.dt.uint8
+FP8X4 = mybir.dt.float8_e4m3fn_x4
+FP4X4 = mybir.dt.float4_e2m1fn_x4
+ALU = mybir.AluOpType
+ACT = mybir.ActivationFunctionType
+
+P = 128
+PACK = 4
+CHUNK = 128
+CHUNKS = I // CHUNK
+LIST_COLS = CHUNK // 16
+
+
+def tile_attend_listedlarger_deliveredplanes_lean_pl_kernel(
+    tc, users, keys_words, keys_scales, qs, msgs, old, offs, offs2, offs3, offs4, out_0, out_1, out_2
+):
+    nc = tc.nc
+    with ExitStack() as ctx:
+        keep = ctx.enter_context(tc.tile_pool(name="keep", bufs=1))
+        ring = ctx.enter_context(tc.tile_pool(name="ring", bufs=4))
+        psum_a = ctx.enter_context(tc.psum_pool(name="psum_a", bufs=3))
+        psum_b = ctx.enter_context(tc.psum_pool(name="psum_b", bufs=2))
+        psum_d = ctx.enter_context(tc.psum_pool(name="psum_d", bufs=2))
+
+        def held(shape, dtype, name):
+            return keep.tile(shape, dtype, name=name, align_bytes=64)
+
+        key_list = held([P, I // 16], U16, "key_list")
+        user_lists = [held([P, Q // 16], U16, "user_list%d" % s) for s in range(2)]
+        place_list = held([P, I // 16], U16, "place_list")
+        key_words = held([P, T], U16, "key_words")
+        key_bytes = held([P, T], U8, "key_bytes")
+        placed = [held([P, M], F32, "placed%d" % t) for t in range(PACK)]
+        for t in range(PACK):
+            (nc.vector if t < 2 else nc.gpsimd).memset(placed[t][:], 0.0)
+
+        users_v = users.rearrange("(p t) u -> p t u", t=PACK)
+        raw = {}
+        for h in range(2):
+            for k in range(2):
+                raw[h, k] = held([P, 2, U // 2], F32, "raw%d%d" % (h, k))
+        msgs_raw = held([P, PACK, E], F32, "msgs_raw")
+        factor = held([P, PACK], F32, "factor")
+        nc.sync.dma_start(key_list[:], offs)
+        nc.sync.dma_start(key_words[:].bitcast(I32), keys_words[0].bitcast(I32))
+        for g in range(4):
+            rows = keys_scales[0, 4 * g : 4 * g + 4, :].bitcast(I32)
+            nc.sync.dma_start(
+                key_bytes[32 * g : 32 * (g + 1), :].bitcast(I32), rows.unsqueeze(0).to_broadcast([8, 4, T // 4])
+            )
+        nc.sync.dma_start(raw[0, 0][:], users_v[:, 0:2, 0 : U // 2])
+        nc.sync.dma_start(raw[0, 1][:], users_v[:, 0:2, U // 2 : U])
+        nc.sync.dma_start(user_lists[1][:], offs3)
+        nc.sync.dma_start(user_lists[0][:], offs2)
+        nc.sync.dma_start(raw[1, 0][:], users_v[:, 2:4, 0 : U // 2])
+        nc.sync.dma_start(raw[1, 1][:], users_v[:, 2:4, U // 2 : U])
+        nc.sync.dma_start(msgs_raw[:], msgs.rearrange("(p r) e -> p r e", r=PACK))
+        nc.sync.dma_start(factor[:], qs.rearrange("(p r) one -> p (r one)", r=PACK))
+        nc.sync.dma_start(place_list[:], offs4)
+        old_v = old.rearrange("(p t) m -> p t m", t=PACK)
+        total = [held([P, 2, M], F32, "total%d" % h) for h in range(2)]
+        for h in range(2):
+            nc.sync.dma_start(total[h][:], old_v[:, 2 * h : 2 * h + 2, :])
+
+        kw = [held([P, I // 2], U16, "kw%d" % k) for k in range(2)]
+        ks = [held([P, I // 2], U8, "ks%d" % k) for k in range(2)]
+
+        def gather_keys(k):
+            part = key_list[:, k * 16 : (k + 1) * 16]
+            nc.vector.tensor_copy(kw[k][:], key_words[:].indirect(part))
+            nc.vector.tensor_copy(ks[k][:], key_bytes[:].indirect(part))
+
+        gather_keys(0)
+        gather_keys(1)
+        pairs = [held([P, U], U32, "pairs%d" % h) for h in range(2)]
+        for h in range(2):
+            for k in range(2):
+                dst = pairs[h][:, k * (U // 2) : (k + 1) * (U // 2)].bitcast(BF16).rearrange("p (u t) -> p u t", t=2)
+                src = raw[h, k][:].rearrange("p t u -> p u t")
+                if (h, k) == (0, 1):
+                    nc.vector.tensor_copy(dst, src)
+                else:
+                    nc.scalar.activation(dst, src, ACT.Copy)
+        picked = [held([P, 2, Q], U32, "picked%d" % s) for s in range(2)]
+        for h in range(2):
+            for s in (1, 0):
+                nc.vector.tensor_copy(picked[s][:, h, :], pairs[h][:].indirect(user_lists[s][:]))
+        user_codes = [held([P, Q], U32, "user_codes%d" % s) for s in range(2)]
+        user_scales = [held([P, Q], U8, "user_scales%d" % s) for s in range(2)]
+        woven = [held([P, 2 * Q], U32, "woven%d" % s) for s in range(2)]
+        for s in (1, 0):
+            nc.scalar.copy(
+                woven[s][:].rearrange("p (r a b h) -> p a r b h", r=PACK, b=2, h=2),
+                picked[s][:].rearrange("p h (a b r) -> p a r b h", r=PACK, b=2),
+            )
+        for s in (1, 0):
+            nc.vector.quantize_mx(out=user_codes[s][:].bitcast(FP8X4), scales=user_scales[s][:], in_=woven[s][:].bitcast(BF16))
+
+        msgs_bf = held([P, PACK * E], BF16, "woven0")
+        msgs_codes = held([P, E], U32, "msgs_codes")
+        msgs_scales = held([P, E], U8, "msgs_scales")
+
+        def round_msgs():
+            dst = msgs_bf[:].rearrange("p (t m r) -> p m t r", t=PACK, r=PACK)
+            src = msgs_raw[:].rearrange("p r (m t) -> p m t r", t=PACK)
+            for k, engine in enumerate(["vector"]):
+                n = P // 1
+                part = slice(k * n, (k + 1) * n)
+                if engine == "vector":
+                    nc.vector.tensor_copy(dst[:, part], src[:, part])
+                elif engine == "gpsimd":
+                    nc.gpsimd.tensor_copy(dst[:, part], src[:, part])
+                else:
+                    nc.scalar.copy(dst[:, part], src[:, part])
+
+        def quantize_msgs():
+            nc.vector.quantize_mx(out=msgs_codes[:].bitcast(FP8X4), scales=msgs_scales[:], in_=msgs_bf[:])
+
+        def scores(s, c, bank):
+            slots = slice(c % 2 * CHUNK, (c % 2 + 1) * CHUNK)
+            for r in range(PACK):
+                rows = slice(r * P, (r + 1) * P)
+                nc.tensor.matmul_mx(
+                    out=bank[:, r, :],
+                    lhsT=user_codes[s][:, rows].bitcast(FP8X4),
+                    lhsT_scale=user_scales[s][:, rows],
+                    rhs=kw[c // 2][:, slots].bitcast(FP4X4),
+                    rhs_scale=ks[c // 2][:, slots],
+                    start=True,
+                    stop=True,
+                )
+
+        dl = [held([P, PACK, I // 2], F32, "dl%d" % k) for k in range(2)]
+        b_sb, s_sb, w_sb, wq = {}, {}, {}, {}
+
+        def stage_b(c):
+            bank = psum_b.tile([P, PACK, CHUNK], F32, name="bank_b")
+            scores(1, c, bank)
+            b_sb[c] = held([P, CHUNK, PACK], F32, "b_sb%d" % c)
+            nc.scalar.copy(b_sb[c][:], bank[:].rearrange("p r n -> p n r"))
+
+        def stage_max(c):
+            bank = psum_a.tile([P, PACK, CHUNK], F32, name="bank_a")
+            scores(0, c, bank)
+            s_sb[c] = ring.tile([P, CHUNK, PACK], F32, name="s_sb")
+            nc.vector.tensor_tensor(s_sb[c][:], bank[:].rearrange("p r n -> p n r"), b_sb[c][:], ALU.max)
+            w_sb[c] = ring.tile([P, CHUNK, PACK], F32, name="w_sb")
+            nc.scalar.activation(w_sb[c][:], s_sb[c][:], ACT.Sigmoid)
+
+        def stage_mult(c):
+            wq[c] = ring.tile([P, CHUNK, PACK], BF16, name="wq", align_bytes=64)
+            nc.vector.tensor_tensor(
+                wq[c][:], w_sb[c][:], factor[:].unsqueeze(1).to_broadcast([P, CHUNK, PACK]), ALU.mult
+            )
+
+        def stage_dl(c):
+            codes = ring.tile([P, CHUNK], U32, name="wq_codes", align_bytes=64)
+            scales = ring.tile([P, CHUNK], U8, name="wq_scales", align_bytes=64)
+            nc.vector.quantize_mx(out=codes[:].bitcast(FP8X4), scales=scales[:], in_=wq[c][:].rearrange("p n r -> p (n r)"))
+            bank = psum_d.tile([P, PACK, CHUNK], F32, name="bank_d")
+            for t in range(PACK):
+                cols = slice(t * P, (t + 1) * P)
+                nc.tensor.matmul_mx(
+                    out=bank[:, t, :],
+                    lhsT=msgs_codes[:, cols].bitcast(FP8X4),
+                    lhsT_scale=msgs_scales[:, cols],
+                    rhs=codes[:].bitcast(FP8X4),
+                    rhs_scale=scales[:],
+                    start=True,
+                    stop=True,
+                )
+            nc.scalar.copy(dl[c // 2][:, :, c % 2 * CHUNK : (c % 2 + 1) * CHUNK], bank[:])
+
+        def scatter(engine, t, c0, c1):
+            window = placed[t][:].indirect(place_list[:, c0 * LIST_COLS : c1 * LIST_COLS])
+            src = dl[c0 // 2][:, t, c0 % 2 * CHUNK : (c0 % 2 + c1 - c0) * CHUNK]
+            if engine == "vector":
+                nc.vector.tensor_copy(window, src)
+            else:
+                nc.scalar.activation(window, src, ACT.Copy)
+
+        stage_b(0)
+        round_msgs()
+        for step in range(CHUNKS + 2):
+            if step < CHUNKS:
+                stage_max(step)
+            if step + 1 < CHUNKS:
+                stage_b(step + 1)
+            if step == 0:
+                quantize_msgs()
+            if 0 <= step - 1 < CHUNKS:
+                stage_mult(step - 1)
+            if 0 <= step - 2 < CHUNKS:
+                stage_dl(step - 2)
+
+        out_v = out_0.rearrange("(p t) m -> p t m", t=PACK)
+        rounded = held([P, M, 2, 2], BF16, "rounded")
+        y_codes = held([P, M], U32, "y_codes")
+        y_scales = held([P, M], U8, "y_scales")
+
+        def add(t, cols, engine=nc.vector):
+            plane = total[t // 2][:, t % 2, cols]
+            engine.tensor_tensor(plane, plane, placed[t][:, cols], ALU.add)
+            nc.sync.dma_start(out_v[:, t, cols], plane)
+
+        def round_pair(engine, h, cols):
+            src = total[h][:, :, cols].rearrange("p j m -> p m j")
+            if engine == "vector":
+                nc.vector.tensor_copy(rounded[:, cols, h, :], src)
+            else:
+                nc.scalar.copy(rounded[:, cols, h, :], src)
+
+        words_v = out_1[0].rearrange("p m t -> p (m t)").bitcast(I32)
+
+        def finish(cols):
+            nc.vector.quantize_mx(
+                out=y_codes[:, cols].bitcast(FP8X4),
+                scales=y_scales[:, cols],
+                in_=rounded[:, cols].rearrange("p m h j -> p (m h j)"),
+            )
+            nc.sync.dma_start(words_v[:, cols], y_codes[:, cols].bitcast(I32))
+
+        halves = [slice(0, M // 2), slice(M // 2, M)]
+        scatter("vector", 0, 0, 2)
+        scatter("scalar", 1, 0, 2)
+        scatter("vector", 0, 2, 4)
+        scatter("scalar", 1, 2, 4)
+        scatter("scalar", 2, 0, 2)
+        scatter("scalar", 2, 2, 4)
+        add(0, slice(0, M))
+        scatter("vector", 3, 0, 2)
+        add(1, slice(0, M))
+        round_pair("vector", 0, slice(0, M))
+        scatter("scalar", 3, 2, 4)
+        add(2, slice(0, M))
+        for cols in halves:
+            add(3, cols)
+        round_pair("scalar", 1, halves[0])
+        round_pair("vector", 1, halves[1])
+        finish(halves[1])
+        finish(halves[0])
+        for r in range(4):
+            nc.sync.dma_start(out_2[0, r:16:4, :].bitcast(I32), y_scales[r:P:32, :].bitcast(I32))

@@ -20,7 +20,10 @@ P = 128
 PACK = 4
 CHUNK = 128
 CHUNKS = I // CHUNK
-LIST_COLS = CHUNK // 16
+
+
+def part(k, n, size):
+    return slice(k * size // n, (k + 1) * size // n)
 
 
 def tile_attend_listedlarger_deliveredplanes_lean_pl_kernel(
@@ -29,10 +32,9 @@ def tile_attend_listedlarger_deliveredplanes_lean_pl_kernel(
     nc = tc.nc
     with ExitStack() as ctx:
         keep = ctx.enter_context(tc.tile_pool(name="keep", bufs=1))
-        ring = ctx.enter_context(tc.tile_pool(name="ring", bufs=4))
         psum_a = ctx.enter_context(tc.psum_pool(name="psum_a", bufs=3))
         psum_b = ctx.enter_context(tc.psum_pool(name="psum_b", bufs=2))
-        psum_d = ctx.enter_context(tc.psum_pool(name="psum_d", bufs=2))
+        psum_d = ctx.enter_context(tc.psum_pool(name="psum_d", bufs=3))
 
         def held(shape, dtype, name):
             return keep.tile(shape, dtype, name=name, align_bytes=64)
@@ -42,17 +44,20 @@ def tile_attend_listedlarger_deliveredplanes_lean_pl_kernel(
         place_list = held([P, I // 16], U16, "place_list")
         key_words = held([P, T], U16, "key_words")
         key_bytes = held([P, T], U8, "key_bytes")
+
         placed = [held([P, M], F32, "placed%d" % t) for t in range(PACK)]
         for t in range(PACK):
-            (nc.vector if t < 2 else nc.gpsimd).memset(placed[t][:], 0.0)
+            (nc.vector if t < 3 else nc.gpsimd).memset(placed[t][:], 0.0)
 
         users_v = users.rearrange("(p t) u -> p t u", t=PACK)
-        raw = {}
-        for h in range(2):
-            for k in range(2):
-                raw[h, k] = held([P, 2, U // 2], F32, "raw%d%d" % (h, k))
-        msgs_raw = held([P, PACK, E], F32, "msgs_raw")
+        msgs_v = msgs.rearrange("(p r) e -> p r e", r=PACK)
+        old_v = old.rearrange("(p t) m -> p t m", t=PACK)
+        out_v = out_0.rearrange("(p t) m -> p t m", t=PACK)
+        raw = {(h, k): held([P, 2, U // 2], F32, "raw%d%d" % (h, k)) for h in range(2) for k in range(2)}
+        msgs_raw = [held([P, PACK, E // 2], F32, "msgs_raw%d" % k) for k in range(2)]
         factor = held([P, PACK], F32, "factor")
+        total = [held([P, PACK, M // 2], F32, "total%d" % k) for k in range(2)]
+
         nc.sync.dma_start(key_list[:], offs)
         nc.sync.dma_start(key_words[:].bitcast(I32), keys_words[0].bitcast(I32))
         for g in range(4):
@@ -60,34 +65,28 @@ def tile_attend_listedlarger_deliveredplanes_lean_pl_kernel(
             nc.sync.dma_start(
                 key_bytes[32 * g : 32 * (g + 1), :].bitcast(I32), rows.unsqueeze(0).to_broadcast([8, 4, T // 4])
             )
-        nc.sync.dma_start(raw[0, 0][:], users_v[:, 0:2, 0 : U // 2])
-        nc.sync.dma_start(raw[0, 1][:], users_v[:, 0:2, U // 2 : U])
+        for k in range(2):
+            nc.sync.dma_start(raw[0, k][:], users_v[:, 0:2, part(k, 2, U)])
         nc.sync.dma_start(user_lists[1][:], offs3)
         nc.sync.dma_start(user_lists[0][:], offs2)
-        nc.sync.dma_start(raw[1, 0][:], users_v[:, 2:4, 0 : U // 2])
-        nc.sync.dma_start(raw[1, 1][:], users_v[:, 2:4, U // 2 : U])
-        nc.sync.dma_start(msgs_raw[:], msgs.rearrange("(p r) e -> p r e", r=PACK))
+        for k in range(2):
+            nc.sync.dma_start(raw[1, k][:], users_v[:, 2:4, part(k, 2, U)])
+        for k in range(2):
+            nc.sync.dma_start(msgs_raw[k][:], msgs_v[:, :, part(k, 2, E)])
         nc.sync.dma_start(factor[:], qs.rearrange("(p r) one -> p (r one)", r=PACK))
         nc.sync.dma_start(place_list[:], offs4)
-        old_v = old.rearrange("(p t) m -> p t m", t=PACK)
-        total = [held([P, 2, M], F32, "total%d" % h) for h in range(2)]
-        for h in range(2):
-            nc.sync.dma_start(total[h][:], old_v[:, 2 * h : 2 * h + 2, :])
+        for k in range(2):
+            nc.sync.dma_start(total[k][:], old_v[:, :, part(k, 2, M)])
 
-        kw = [held([P, I // 2], U16, "kw%d" % k) for k in range(2)]
-        ks = [held([P, I // 2], U8, "ks%d" % k) for k in range(2)]
+        slot_words = held([P, I], U16, "slot_words")
+        slot_bytes = held([P, I], U8, "slot_bytes")
+        nc.vector.tensor_copy(slot_words[:], key_words[:].indirect(key_list[:]))
+        nc.vector.tensor_copy(slot_bytes[:], key_bytes[:].indirect(key_list[:]))
 
-        def gather_keys(k):
-            part = key_list[:, k * 16 : (k + 1) * 16]
-            nc.vector.tensor_copy(kw[k][:], key_words[:].indirect(part))
-            nc.vector.tensor_copy(ks[k][:], key_bytes[:].indirect(part))
-
-        gather_keys(0)
-        gather_keys(1)
         pairs = [held([P, U], U32, "pairs%d" % h) for h in range(2)]
         for h in range(2):
             for k in range(2):
-                dst = pairs[h][:, k * (U // 2) : (k + 1) * (U // 2)].bitcast(BF16).rearrange("p (u t) -> p u t", t=2)
+                dst = pairs[h][:, part(k, 2, U)].bitcast(BF16).rearrange("p (u t) -> p u t", t=2)
                 src = raw[h, k][:].rearrange("p t u -> p u t")
                 if (h, k) == (0, 1):
                     nc.vector.tensor_copy(dst, src)
@@ -108,42 +107,35 @@ def tile_attend_listedlarger_deliveredplanes_lean_pl_kernel(
         for s in (1, 0):
             nc.vector.quantize_mx(out=user_codes[s][:].bitcast(FP8X4), scales=user_scales[s][:], in_=woven[s][:].bitcast(BF16))
 
-        msgs_bf = held([P, PACK * E], BF16, "woven0")
-        msgs_codes = held([P, E], U32, "msgs_codes")
+        msgs_bf = held([P, PACK * E], BF16, "msgs_bf")
+        msgs_codes = held([P, E], U32, "woven0")
         msgs_scales = held([P, E], U8, "msgs_scales")
+        msgs_dealt = msgs_bf[:].rearrange("p (t m r) -> p m t r", t=PACK, r=PACK)
 
         def round_msgs():
-            dst = msgs_bf[:].rearrange("p (t m r) -> p m t r", t=PACK, r=PACK)
-            src = msgs_raw[:].rearrange("p r (m t) -> p m t r", t=PACK)
-            for k, engine in enumerate(["vector"]):
-                n = P // 1
-                part = slice(k * n, (k + 1) * n)
-                if engine == "vector":
-                    nc.vector.tensor_copy(dst[:, part], src[:, part])
-                elif engine == "gpsimd":
-                    nc.gpsimd.tensor_copy(dst[:, part], src[:, part])
+            for k in range(2):
+                src = msgs_raw[k][:].rearrange("p r (m t) -> p m t r", t=PACK)
+                if k == 0:
+                    nc.scalar.copy(msgs_dealt[:, part(k, 2, P)], src)
                 else:
-                    nc.scalar.copy(dst[:, part], src[:, part])
-
-        def quantize_msgs():
-            nc.vector.quantize_mx(out=msgs_codes[:].bitcast(FP8X4), scales=msgs_scales[:], in_=msgs_bf[:])
+                    nc.vector.tensor_copy(msgs_dealt[:, part(k, 2, P)], src)
 
         def scores(s, c, bank):
-            slots = slice(c % 2 * CHUNK, (c % 2 + 1) * CHUNK)
+            slots = part(c, CHUNKS, I)
             for r in range(PACK):
-                rows = slice(r * P, (r + 1) * P)
+                rows = part(r, PACK, Q)
                 nc.tensor.matmul_mx(
                     out=bank[:, r, :],
                     lhsT=user_codes[s][:, rows].bitcast(FP8X4),
                     lhsT_scale=user_scales[s][:, rows],
-                    rhs=kw[c // 2][:, slots].bitcast(FP4X4),
-                    rhs_scale=ks[c // 2][:, slots],
+                    rhs=slot_words[:, slots].bitcast(FP4X4),
+                    rhs_scale=slot_bytes[:, slots],
                     start=True,
                     stop=True,
                 )
 
-        dl = [held([P, PACK, I // 2], F32, "dl%d" % k) for k in range(2)]
-        b_sb, s_sb, w_sb, wq = {}, {}, {}, {}
+        dl = {}
+        b_sb, w_sb, wq = {}, {}, {}
 
         def stage_b(c):
             bank = psum_b.tile([P, PACK, CHUNK], F32, name="bank_b")
@@ -154,24 +146,24 @@ def tile_attend_listedlarger_deliveredplanes_lean_pl_kernel(
         def stage_max(c):
             bank = psum_a.tile([P, PACK, CHUNK], F32, name="bank_a")
             scores(0, c, bank)
-            s_sb[c] = ring.tile([P, CHUNK, PACK], F32, name="s_sb")
-            nc.vector.tensor_tensor(s_sb[c][:], bank[:].rearrange("p r n -> p n r"), b_sb[c][:], ALU.max)
-            w_sb[c] = ring.tile([P, CHUNK, PACK], F32, name="w_sb")
-            nc.scalar.activation(w_sb[c][:], s_sb[c][:], ACT.Sigmoid)
+            s_sb = held([P, CHUNK, PACK], F32, "s_sb%d" % c)
+            nc.vector.tensor_tensor(s_sb[:], bank[:].rearrange("p r n -> p n r"), b_sb[c][:], ALU.max)
+            w_sb[c] = held([P, CHUNK, PACK], F32, "w_sb%d" % c)
+            nc.scalar.activation(w_sb[c][:], s_sb[:], ACT.Sigmoid)
 
         def stage_mult(c):
-            wq[c] = ring.tile([P, CHUNK, PACK], BF16, name="wq", align_bytes=64)
+            wq[c] = held([P, CHUNK, PACK], BF16, "wq%d" % c)
             nc.vector.tensor_tensor(
                 wq[c][:], w_sb[c][:], factor[:].unsqueeze(1).to_broadcast([P, CHUNK, PACK]), ALU.mult
             )
 
         def stage_dl(c):
-            codes = ring.tile([P, CHUNK], U32, name="wq_codes", align_bytes=64)
-            scales = ring.tile([P, CHUNK], U8, name="wq_scales", align_bytes=64)
+            codes = held([P, CHUNK], U32, "wq_codes%d" % c)
+            scales = held([P, CHUNK], U8, "wq_scales%d" % c)
             nc.vector.quantize_mx(out=codes[:].bitcast(FP8X4), scales=scales[:], in_=wq[c][:].rearrange("p n r -> p (n r)"))
             bank = psum_d.tile([P, PACK, CHUNK], F32, name="bank_d")
             for t in range(PACK):
-                cols = slice(t * P, (t + 1) * P)
+                cols = part(t, PACK, E)
                 nc.tensor.matmul_mx(
                     out=bank[:, t, :],
                     lhsT=msgs_codes[:, cols].bitcast(FP8X4),
@@ -181,75 +173,73 @@ def tile_attend_listedlarger_deliveredplanes_lean_pl_kernel(
                     start=True,
                     stop=True,
                 )
-            nc.scalar.copy(dl[c // 2][:, :, c % 2 * CHUNK : (c % 2 + 1) * CHUNK], bank[:])
+            if c % 2 == 0:
+                dl[c // 2] = held([P, PACK, I // 2], F32, "s_sb3" if c == 0 else "dl1")
+            nc.scalar.copy(dl[c // 2][:, :, part(c % 2, 2, I // 2)], bank[:])
 
-        def scatter(engine, t, c0, c1):
-            window = placed[t][:].indirect(place_list[:, c0 * LIST_COLS : c1 * LIST_COLS])
-            src = dl[c0 // 2][:, t, c0 % 2 * CHUNK : (c0 % 2 + c1 - c0) * CHUNK]
+        def scatter(engine, t, k):
+            window = placed[t][:].indirect(place_list[:, part(k, 2, I // 16)])
             if engine == "vector":
-                nc.vector.tensor_copy(window, src)
+                nc.vector.tensor_copy(window, dl[k][:, t, :])
             else:
-                nc.scalar.activation(window, src, ACT.Copy)
+                nc.scalar.activation(window, dl[k][:, t, :], ACT.Copy)
 
         stage_b(0)
         round_msgs()
-        for step in range(CHUNKS + 2):
+        for step in range(CHUNKS + 4):
             if step < CHUNKS:
                 stage_max(step)
             if step + 1 < CHUNKS:
                 stage_b(step + 1)
             if step == 0:
-                quantize_msgs()
-            if 0 <= step - 1 < CHUNKS:
-                stage_mult(step - 1)
+                nc.vector.quantize_mx(out=msgs_codes[:].bitcast(FP8X4), scales=msgs_scales[:], in_=msgs_bf[:])
             if 0 <= step - 2 < CHUNKS:
-                stage_dl(step - 2)
+                stage_mult(step - 2)
+            if 0 <= step - 4 < CHUNKS:
+                stage_dl(step - 4)
 
-        out_v = out_0.rearrange("(p t) m -> p t m", t=PACK)
-        rounded = held([P, M, 2, 2], BF16, "rounded")
+        rounded = [held([P, M // 4, PACK], BF16, "rounded%d" % j) for j in range(4)]
         y_codes = held([P, M], U32, "y_codes")
         y_scales = held([P, M], U8, "y_scales")
-
-        def add(t, cols, engine=nc.vector):
-            plane = total[t // 2][:, t % 2, cols]
-            engine.tensor_tensor(plane, plane, placed[t][:, cols], ALU.add)
-            nc.sync.dma_start(out_v[:, t, cols], plane)
-
-        def round_pair(engine, h, cols):
-            src = total[h][:, :, cols].rearrange("p j m -> p m j")
-            if engine == "vector":
-                nc.vector.tensor_copy(rounded[:, cols, h, :], src)
-            else:
-                nc.scalar.copy(rounded[:, cols, h, :], src)
-
         words_v = out_1[0].rearrange("p m t -> p (m t)").bitcast(I32)
 
-        def finish(cols):
+        def add(t, k, engine=nc.vector):
+            plane = total[k][:, t, :]
+            engine.tensor_tensor(plane, plane, placed[t][:, part(k, 2, M)], ALU.add)
+            nc.sync.dma_start(out_v[:, t, part(k, 2, M)], plane)
+
+        def round_quarter(engine, j):
+            src = total[j // 2][:, :, part(j % 2, 2, M // 2)].rearrange("p t m -> p m t")
+            if engine == "vector":
+                nc.vector.tensor_copy(rounded[j][:], src)
+            else:
+                nc.scalar.copy(rounded[j][:], src)
+
+        def finish(j):
+            cols = part(j, 4, M)
             nc.vector.quantize_mx(
                 out=y_codes[:, cols].bitcast(FP8X4),
                 scales=y_scales[:, cols],
-                in_=rounded[:, cols].rearrange("p m h j -> p (m h j)"),
+                in_=rounded[j][:].rearrange("p m t -> p (m t)"),
             )
             nc.sync.dma_start(words_v[:, cols], y_codes[:, cols].bitcast(I32))
 
-        halves = [slice(0, M // 2), slice(M // 2, M)]
-        scatter("vector", 0, 0, 2)
-        scatter("scalar", 1, 0, 2)
-        scatter("vector", 0, 2, 4)
-        scatter("scalar", 1, 2, 4)
-        scatter("scalar", 2, 0, 2)
-        scatter("scalar", 2, 2, 4)
-        add(0, slice(0, M))
-        scatter("vector", 3, 0, 2)
-        add(1, slice(0, M))
-        round_pair("vector", 0, slice(0, M))
-        scatter("scalar", 3, 2, 4)
-        add(2, slice(0, M))
-        for cols in halves:
-            add(3, cols)
-        round_pair("scalar", 1, halves[0])
-        round_pair("vector", 1, halves[1])
-        finish(halves[1])
-        finish(halves[0])
+        scatter("vector", 0, 0)
+        scatter("scalar", 1, 0)
+        scatter("vector", 0, 1)
+        scatter("scalar", 1, 1)
+        scatter("scalar", 2, 1)
+        scatter("scalar", 2, 0)
+        scatter("vector", 3, 0)
+        scatter("vector", 3, 1)
+        for k in range(2):
+            for t in (0, 1, 3, 2):
+                add(t, k)
+        round_quarter("scalar", 0)
+        round_quarter("scalar", 1)
+        round_quarter("vector", 2)
+        round_quarter("scalar", 3)
+        for j in (0, 2, 1, 3):
+            finish(j)
         for r in range(4):
-            nc.sync.dma_start(out_2[0, r:16:4, :].bitcast(I32), y_scales[r:P:32, :].bitcast(I32))
+            (nc.sync if r < 2 else nc.scalar).dma_start(out_2[0, r:16:4, :].bitcast(I32), y_scales[r:P:32, :].bitcast(I32))

@@ -45,6 +45,10 @@ def tile_attend_listedlarger_deliveredplanes_lean_pl_kernel(
         key_words = held([P, T], U16, "key_words")
         key_bytes = held([P, T], U8, "key_bytes")
 
+        warm = held([P, 16], F32, "warm")
+        nc.vector.memset(warm[:, 0:8], 0.0)
+        nc.scalar.activation(warm[:, 8:16], warm[:, 0:8], ACT.Sigmoid)
+
         placed = [held([P, M], F32, "placed%d" % t) for t in range(PACK)]
         for t in range(PACK):
             (nc.vector if t < 3 else nc.gpsimd).memset(placed[t][:], 0.0)

from contextlib import ExitStack

import concourse.mybir as mybir

D, T, I, Q, E, U, M = 512, 2048, 512, 512, 512, 1024, 1024
FLOPS = 2 * (2 * Q * I * D + E * I * Q)

F32 = mybir.dt.float32
BF16 = mybir.dt.bfloat16
I32 = mybir.dt.int32
U32 = mybir.dt.uint32
U16 = mybir.dt.uint16
U8 = mybir.dt.uint8
FP8X4 = mybir.dt.float8_e4m3fn_x4
FP4X4 = mybir.dt.float4_e2m1fn_x4
ALU = mybir.AluOpType
ACT = mybir.ActivationFunctionType

P = 128
PACK = 4
CHUNK = 128
CHUNKS = I // CHUNK


def part(k, n, size):
    return slice(k * size // n, (k + 1) * size // n)


def tile_attend_listedlarger_deliveredplanes_lean_pl_kernel(
    tc, users, keys_words, keys_scales, qs, msgs, old, offs, offs2, offs3, offs4, out_0, out_1, out_2
):
    nc = tc.nc
    with ExitStack() as ctx:
        keep = ctx.enter_context(tc.tile_pool(name="keep", bufs=1))
        psum_a = ctx.enter_context(tc.psum_pool(name="psum_a", bufs=3))
        psum_b = ctx.enter_context(tc.psum_pool(name="psum_b", bufs=2))
        psum_d = ctx.enter_context(tc.psum_pool(name="psum_d", bufs=3))

        def held(shape, dtype, name):
            return keep.tile(shape, dtype, name=name, align_bytes=64)

        key_list = held([P, I // 16], U16, "key_list")
        user_lists = [held([P, Q // 16], U16, "user_list%d" % s) for s in range(2)]
        place_list = held([P, I // 16], U16, "place_list")
        key_words = held([P, T], U16, "key_words")
        key_bytes = held([P, T], U8, "key_bytes")

        warm = held([P, 16], F32, "warm")
        nc.vector.memset(warm[:, 0:8], 0.0)
        nc.scalar.activation(warm[:, 8:16], warm[:, 0:8], ACT.Sigmoid)

        placed = [held([P, M], F32, "placed%d" % t) for t in range(PACK)]
        for t in range(PACK):
            (nc.vector if t < 3 else nc.gpsimd).memset(placed[t][:], 0.0)

        users_v = users.rearrange("(p t) u -> p t u", t=PACK)
        msgs_v = msgs.rearrange("(p r) e -> p r e", r=PACK)
        old_v = old.rearrange("(p t) m -> p t m", t=PACK)
        out_v = out_0.rearrange("(p t) m -> p t m", t=PACK)
        raw = {(h, k): held([P, 2, U // 2], F32, "raw%d%d" % (h, k)) for h in range(2) for k in range(2)}
        msgs_raw = [held([P, PACK, E // 2], F32, "msgs_raw%d" % k) for k in range(2)]
        factor = held([P, PACK], F32, "factor")
        total = [held([P, PACK, M // 2], F32, "total%d" % k) for k in range(2)]

        nc.sync.dma_start(key_list[:], offs)
        nc.sync.dma_start(key_words[:].bitcast(I32), keys_words[0].bitcast(I32))
        for g in range(4):
            rows = keys_scales[0, 4 * g : 4 * g + 4, :].bitcast(I32)
            nc.sync.dma_start(
                key_bytes[32 * g : 32 * (g + 1), :].bitcast(I32), rows.unsqueeze(0).to_broadcast([8, 4, T // 4])
            )
        for k in range(2):
            nc.sync.dma_start(raw[0, k][:], users_v[:, 0:2, part(k, 2, U)])
        nc.sync.dma_start(user_lists[1][:], offs3)
        nc.sync.dma_start(user_lists[0][:], offs2)
        for k in range(2):
            nc.sync.dma_start(raw[1, k][:], users_v[:, 2:4, part(k, 2, U)])
        for k in range(2):
            nc.sync.dma_start(msgs_raw[k][:], msgs_v[:, :, part(k, 2, E)])
        nc.sync.dma_start(factor[:], qs.rearrange("(p r) one -> p (r one)", r=PACK))
        nc.sync.dma_start(place_list[:], offs4)
        for k in range(2):
            nc.sync.dma_start(total[k][:], old_v[:, :, part(k, 2, M)])

        slot_words = held([P, I], U16, "slot_words")
        slot_bytes = held([P, I], U8, "slot_bytes")
        nc.vector.tensor_copy(slot_words[:], key_words[:].indirect(key_list[:]))
        nc.vector.tensor_copy(slot_bytes[:], key_bytes[:].indirect(key_list[:]))

        pairs = [held([P, U], U32, "pairs%d" % h) for h in range(2)]
        for h in range(2):
            for k in range(2):
                dst = pairs[h][:, part(k, 2, U)].bitcast(BF16).rearrange("p (u t) -> p u t", t=2)
                src = raw[h, k][:].rearrange("p t u -> p u t")
                if (h, k) == (0, 1):
                    nc.vector.tensor_copy(dst, src)
                else:
                    nc.scalar.activation(dst, src, ACT.Copy)
        picked = [held([P, 2, Q], U32, "picked%d" % s) for s in range(2)]
        for h in range(2):
            for s in (1, 0):
                nc.vector.tensor_copy(picked[s][:, h, :], pairs[h][:].indirect(user_lists[s][:]))
        user_codes = [held([P, Q], U32, "user_codes%d" % s) for s in range(2)]
        user_scales = [held([P, Q], U8, "user_scales%d" % s) for s in range(2)]
        woven = [held([P, 2 * Q], U32, "woven%d" % s) for s in range(2)]
        for s in (1, 0):
            nc.scalar.copy(
                woven[s][:].rearrange("p (r a b h) -> p a r b h", r=PACK, b=2, h=2),
                picked[s][:].rearrange("p h (a b r) -> p a r b h", r=PACK, b=2),
            )
        for s in (1, 0):
            nc.vector.quantize_mx(out=user_codes[s][:].bitcast(FP8X4), scales=user_scales[s][:], in_=woven[s][:].bitcast(BF16))

        msgs_bf = held([P, PACK * E], BF16, "msgs_bf")
        msgs_codes = held([P, E], U32, "woven0")
        msgs_scales = held([P, E], U8, "msgs_scales")
        msgs_dealt = msgs_bf[:].rearrange("p (t m r) -> p m t r", t=PACK, r=PACK)

        def round_msgs():
            for k in range(2):
                src = msgs_raw[k][:].rearrange("p r (m t) -> p m t r", t=PACK)
                if k == 0:
                    nc.scalar.copy(msgs_dealt[:, part(k, 2, P)], src)
                else:
                    nc.vector.tensor_copy(msgs_dealt[:, part(k, 2, P)], src)

        def scores(s, c, bank):
            slots = part(c, CHUNKS, I)
            for r in range(PACK):
                rows = part(r, PACK, Q)
                nc.tensor.matmul_mx(
                    out=bank[:, r, :],
                    lhsT=user_codes[s][:, rows].bitcast(FP8X4),
                    lhsT_scale=user_scales[s][:, rows],
                    rhs=slot_words[:, slots].bitcast(FP4X4),
                    rhs_scale=slot_bytes[:, slots],
                    start=True,
                    stop=True,
                )

        dl = {}
        b_sb, w_sb, wq = {}, {}, {}

        def stage_b(c):
            bank = psum_b.tile([P, PACK, CHUNK], F32, name="bank_b")
            scores(1, c, bank)
            b_sb[c] = held([P, CHUNK, PACK], F32, "b_sb%d" % c)
            nc.scalar.copy(b_sb[c][:], bank[:].rearrange("p r n -> p n r"))

        def stage_max(c):
            bank = psum_a.tile([P, PACK, CHUNK], F32, name="bank_a")
            scores(0, c, bank)
            s_sb = held([P, CHUNK, PACK], F32, "s_sb%d" % c)
            nc.vector.tensor_tensor(s_sb[:], bank[:].rearrange("p r n -> p n r"), b_sb[c][:], ALU.max)
            w_sb[c] = held([P, CHUNK, PACK], F32, "w_sb%d" % c)
            nc.scalar.activation(w_sb[c][:], s_sb[:], ACT.Sigmoid)

        def stage_mult(c):
            wq[c] = held([P, CHUNK, PACK], BF16, "wq%d" % c)
            nc.vector.tensor_tensor(
                wq[c][:], w_sb[c][:], factor[:].unsqueeze(1).to_broadcast([P, CHUNK, PACK]), ALU.mult
            )

        def stage_dl(c):
            codes = held([P, CHUNK], U32, "wq_codes%d" % c)
            scales = held([P, CHUNK], U8, "wq_scales%d" % c)
            nc.vector.quantize_mx(out=codes[:].bitcast(FP8X4), scales=scales[:], in_=wq[c][:].rearrange("p n r -> p (n r)"))
            bank = psum_d.tile([P, PACK, CHUNK], F32, name="bank_d")
            for t in range(PACK):
                cols = part(t, PACK, E)
                nc.tensor.matmul_mx(
                    out=bank[:, t, :],
                    lhsT=msgs_codes[:, cols].bitcast(FP8X4),
                    lhsT_scale=msgs_scales[:, cols],
                    rhs=codes[:].bitcast(FP8X4),
                    rhs_scale=scales[:],
                    start=True,
                    stop=True,
                )
            if c % 2 == 0:
                dl[c // 2] = held([P, PACK, I // 2], F32, "s_sb3" if c == 0 else "dl1")
            nc.scalar.copy(dl[c // 2][:, :, part(c % 2, 2, I // 2)], bank[:])

        def scatter(engine, t, k):
            window = placed[t][:].indirect(place_list[:, part(k, 2, I // 16)])
            if engine == "vector":
                nc.vector.tensor_copy(window, dl[k][:, t, :])
            else:
                nc.scalar.activation(window, dl[k][:, t, :], ACT.Copy)

        stage_b(0)
        round_msgs()
        for step in range(CHUNKS + 4):
            if step < CHUNKS:
                stage_max(step)
            if step + 1 < CHUNKS:
                stage_b(step + 1)
            if step == 0:
                nc.vector.quantize_mx(out=msgs_codes[:].bitcast(FP8X4), scales=msgs_scales[:], in_=msgs_bf[:])
            if 0 <= step - 2 < CHUNKS:
                stage_mult(step - 2)
            if 0 <= step - 4 < CHUNKS:
                stage_dl(step - 4)

        rounded = [held([P, M // 4, PACK], BF16, "rounded%d" % j) for j in range(4)]
        y_codes = held([P, M], U32, "y_codes")
        y_scales = held([P, M], U8, "y_scales")
        words_v = out_1[0].rearrange("p m t -> p (m t)").bitcast(I32)

        def add(t, k, engine=nc.vector):
            plane = total[k][:, t, :]
            engine.tensor_tensor(plane, plane, placed[t][:, part(k, 2, M)], ALU.add)
            nc.sync.dma_start(out_v[:, t, part(k, 2, M)], plane)

        def round_quarter(engine, j):
            src = total[j // 2][:, :, part(j % 2, 2, M // 2)].rearrange("p t m -> p m t")
            if engine == "vector":
                nc.vector.tensor_copy(rounded[j][:], src)
            else:
                nc.scalar.copy(rounded[j][:], src)

        def finish(j):
            cols = part(j, 4, M)
            nc.vector.quantize_mx(
                out=y_codes[:, cols].bitcast(FP8X4),
                scales=y_scales[:, cols],
                in_=rounded[j][:].rearrange("p m t -> p (m t)"),
            )
            nc.sync.dma_start(words_v[:, cols], y_codes[:, cols].bitcast(I32))

        scatter("vector", 0, 0)
        scatter("scalar", 1, 0)
        scatter("vector", 0, 1)
        scatter("scalar", 1, 1)
        scatter("scalar", 2, 1)
        scatter("scalar", 2, 0)
        scatter("vector", 3, 0)
        scatter("vector", 3, 1)
        for k in range(2):
            for t in (0, 1, 3, 2):
                add(t, k)
        round_quarter("scalar", 0)
        round_quarter("scalar", 1)
        round_quarter("vector", 2)
        round_quarter("scalar", 3)
        for j in (0, 2, 1, 3):
            finish(j)
        for r in range(4):
            (nc.sync if r < 2 else nc.scalar).dma_start(out_2[0, r:16:4, :].bitcast(I32), y_scales[r:P:32, :].bitcast(I32))
